import numpy as np, ml_dtypes
CORES = [10,34,74,98]
N = 4
import mx_ref
BF = ml_dtypes.bfloat16
def entries(a):
    return np.ascontiguousarray(a.T).reshape(-1)
def table(e):
    return np.ascontiguousarray(np.reshape(e, (-1, 16)).T).astype(np.int32)
def f(rng, *shape):
    return mx_ref.flush((rng.standard_normal(shape, dtype=np.float32) * np.exp2(rng.integers(-2, 3, shape[:-1] + (1,)))).astype(BF))
def wide(rng, *shape, cols=0):
    v = rng.standard_normal(shape, dtype=np.float32) * np.exp2(rng.integers(-12, 13, shape)).astype(np.float32)
    if cols: v *= np.repeat(np.exp2(rng.integers(-cols, cols + 1, shape[:-2] + (1, shape[-1] // 4))) * (rng.random(shape[:-2] + (1, shape[-1] // 4)) > 0.0625), 4, axis=-1).astype(np.float32)
    return mx_ref.flush(v.astype(BF))
SH, CH, RD = 160, 64, 4
def lists(rng, same=False, apart=False, ends=False):
    a = []
    for r in range(N):
        p = rng.permutation(SH); e = []
        for t in range(1, RD):
            if same: c = p[:CH]
            elif apart: c = p[np.arange(CH * (t - 1), CH * t) % SH]
            elif ends: c = np.concatenate([[0, SH - 1], 1 + rng.permutation(SH - 2)[:CH - 2]])
            else: c = rng.permutation(SH)[:CH]
            e.append(rng.permutation(c))
        a.append(table(np.concatenate(e)))
    return {"idx": np.stack(a)}
def setup_inputs(rng):
    return {"wm": f(rng, N, 128, 4 * SH), "dl": f(rng, N, 128, (RD - 1) * 4 * CH), **lists(rng), "x": f(rng, N, 128, RD * 512)}
def setup_inputs_same(rng):
    return {**setup_inputs(rng), **lists(rng, same=True)}
def setup_inputs_apart(rng):
    return {**setup_inputs(rng), **lists(rng, apart=True)}
def setup_inputs_ends(rng):
    return {**setup_inputs(rng), **lists(rng, ends=True)}
def setup_inputs_big(rng):
    d = setup_inputs(rng); d["dl"] = (d["dl"].astype(np.float32) * np.float32(256)).astype(BF); return d
def setup_inputs_spread(rng):
    d = setup_inputs(rng); d["wm"] = wide(rng, N, 128, 4 * SH, cols=8); d["dl"] = wide(rng, N, 128, (RD - 1) * 4 * CH, cols=8); return d
def check_inputs(d):
    b = []
    for r in range(N):
        e = entries(d["idx"][r])
        if e.min() < 0 or e.max() >= SH: b.append("idx: range")
        for t in range(1, RD):
            if len(set(e[CH * (t - 1):CH * t].tolist())) != CH: b.append("idx: a column twice in one round")
    return b
def reference(wm, dl, idx, x):
    W = []
    for q in range(N):
        m = wm[q].reshape(128, SH, 4).copy(); d = dl[q].reshape(128, (RD - 1) * CH, 4); e = entries(idx[q])
        W.append([mx_ref.quantize(wm[q])])
        for t in range(1, RD):
            s = slice(CH * (t - 1), CH * t)
            m[:, e[s]] = (m[:, e[s]].astype(np.float32) + np.float32(0.25) * d[:, s].astype(np.float32)).astype(BF)
            W[q].append(mx_ref.quantize(m.reshape(128, 4 * SH).copy()))
    y = np.zeros((N, 128, RD * N * SH), np.float32)
    for r in range(N):
        for t in range(RD):
            X = mx_ref.quantize(np.ascontiguousarray(x[r][:, 512 * t:512 * t + 512]))
            for q in range(N):
                k = t * N + q
                y[r][:, SH * k:SH * k + SH] = mx_ref.matmul(X, W[q][t])
    return {"y": y}

from concourse.bass import DstId, RemoteDMATransfer
from concourse.mybir import dt, AluOpType, AxisListType, ActivationFunctionType

SH, CH, RD = 160, 64, 4
SLOT = SH + (RD - 1) * CH
NR = 4
NT = NR * (RD - 1)

SCRATCH = {
    "C": ("sbuf", [128, NR * SLOT], "float8_e4m3fn_x4"),
    "CS": ("sbuf", [128, NR * SLOT], "uint8"),
    "XB": ("sbuf", [128, RD * 512], "bfloat16"),
    "XC": ("sbuf", [128, RD * 128], "float8_e4m3fn_x4"),
    "XS": ("sbuf", [128, RD * 128], "uint8"),
    "M": ("sbuf", [128, 4 * SLOT], "bfloat16"),
    "DL": ("sbuf", [128, (RD - 1) * 4 * CH], "bfloat16"),
    "DQ": ("sbuf", [128, (RD - 1) * 4 * CH], "bfloat16"),
    "IDX": ("sbuf", [128, 12], "int32"),
    "I16": ("sbuf", [128, 12], "uint16"),
    "I4": ("sbuf", [128, 4], "uint16"),
    "OF2": ("sbuf", [128, 4], "uint16"),
    "OF3": ("sbuf", [128, 4], "uint16"),
    "PT": ("sbuf", [128, 648], "float32"),
    "VAL": ("sbuf", [128, 192], "float32"),
    "MI": ("sbuf", [128, 64], "int32"),
    "MJ": ("sbuf", [128, 64], "int32"),
    "MK": ("sbuf", [128, 64], "float32"),
    "GM2": ("sbuf", [128, 64], "float32"),
    "GM3": ("sbuf", [128, 64], "float32"),
    "RD2": ("sbuf", [128, 4], "float32"),
    "RD3": ("sbuf", [128, 4], "float32"),
    "PI": ("sbuf", [128, 1], "int32"),
    "PA": ("sbuf", [128, 1], "int32"),
    "PB": ("sbuf", [128, 1], "int32"),
    "PF": ("sbuf", [128, 1], "float32"),
    "PG": ("sbuf", [128, 1], "float32"),
    "KB": ("sbuf", [128, 10], "float32"),
    "LF": ("sbuf", [128, 10], "float32"),
    "LST": ("sbuf", [128, 10], "uint16"),
    "VP": ("sbuf", [128, 160], "float32"),
    "VT": ("sbuf", [128, 160], "float32"),
    "OL": ("sbuf", [128, 5], "uint16"),
    "land": ("dram", [NR, 128, 5], "uint16"),
    "OFF": ("sbuf", [128, NR * 40], "uint16"),
    "R": ("sbuf", [128, NT * SLOT], "float32"),
    "Y": ("sbuf", [128, RD * NR * SH], "float32"),
}
for _b in range(8):
    SCRATCH["ps%d" % _b] = ("psum", [128, 512], "float32")

SEMAPHORES = ["ldw", "ldi", "ldd", "ldx", "sv", "ss", "sp", "sg", "hc", "hs", "lsem", "own", "st"]
SEMAPHORES += ["aw%d" % _q for _q in range(NR)] + ["ad%d" % _q for _q in range(NR)]
SEMAPHORES += ["al%d" % _q for _q in range(NR)] + ["rp%d" % _q for _q in range(NR)]


def helper_table(T, topo, r):
    me = T.cores[r]
    dests = [(r + k) % NR for k in range(1, NR)]
    cand = {}
    for d in dests:
        cand[d] = [c for c in topo.cores_of(me)
                   if topo.die(c) != topo.die(me) and T.rank_of(c) is None and topo.may_write(c, T.cores[d])]
    out, used = {}, []
    for d in sorted(dests, key=lambda e: len(cand[e])):
        free = [c for c in cand[d] if c not in used]
        free.sort(key=lambda c: sum(1 for e in dests if c in cand[e]))
        out[d] = free[0]
        used.append(free[0])
    return out


def codes(T, a, b):
    return T.C[:, a:b].bitcast(dt.uint8)


def helper_program(g, core, T, topo):
    for r in range(NR):
        for d, c in helper_table(T, topo, r).items():
            if c != core:
                continue
            dst = T.cores[d]
            m = topo.mask(core, dst)
            rid, pid, _ = topo.addr(dst)
            b = SLOT * r
            n_on = len(topo.engines(T.cores[r], core))
            g.wait_ge(T.sem.hc, n_on)
            g.remote_dma(out_ap=codes(T, b, b + SH), in_ap=codes(T, b, b + SH), remote_sem=T.sem["aw%d" % r],
                         local_sem=T.sem.lsem, pid=pid, routing_id=rid, dma_engine_mask=m)
            g.wait_ge(T.sem.hs, n_on)
            g.remote_dma(out_ap=T.CS[:, b:b + SH], in_ap=T.CS[:, b:b + SH], remote_sem=T.sem["aw%d" % r],
                         local_sem=T.sem.lsem, pid=pid, routing_id=rid, dma_engine_mask=m)
            g.wait_ge(T.sem.lsem, 2 * len(topo.engines(core, dst)))


def rank_program(g, core, T, topo):
    rank = T.rank_of(core)
    if rank is None:
        helper_program(g, core, T, topo)
        return
    add, mult = AluOpType.add, AluOpType.mult
    Copy = ActivationFunctionType.Copy
    eng = {"g": g, "v": g.vector, "s": g.scalar, "p": g.tensor, "y": g.sync}
    cnt = {"sv": 0, "ss": 0, "sp": 0, "sg": 0}
    seen = {}

    def need(q, *toks):
        for t in toks:
            if t is not None and seen.get((q, t[0]), 0) < t[1]:
                eng[q].wait_ge(T.sem[t[0]], t[1])
                seen[(q, t[0])] = t[1]

    def tok(sem, ins):
        ins.then_inc(T.sem[sem], 1)
        cnt[sem] += 1
        return (sem, cnt[sem])

    V, S = g.vector, g.scalar
    order = [(rank - k) % NR for k in range(1, NR)]
    dests = [(rank + k) % NR for k in range(1, NR)]
    base = SLOT * rank

    g.sync.dma_start(T.M[:, 0:4 * SH], T.wm[:]).then_inc(T.sem.ldw, 16)
    for k in range(8):
        e = g.scalar if k % 2 else g.sync
        e.dma_start(T.IDX[16 * k:16 * k + 16, :], T.idx[:]).then_inc(T.sem.ldi, 16)
    g.scalar.dma_start(T.DL[:], T.dl[:]).then_inc(T.sem.ldd, 16)
    g.sync.dma_start(T.XB[:], T.x[:]).then_inc(T.sem.ldx, 16)
    w_w, w_i, w_d, w_x = ("ldw", 16), ("ldi", 128), ("ldd", 16), ("ldx", 16)

    t_mi = tok("sg", g.iota(T.MI[:], [[1, 64]], 128, -1))
    t_pi = tok("sg", g.iota(T.PI[:], [[1, 1]], 0, 1))
    t_kb = tok("sg", g.iota(T.KB[:], [[16, 5], [2, 2]], 0, 0, allow_small_or_imprecise_dtypes=True))
    t_pt = tok("sg", g.iota(T.PT[:, 0:SH], [[1, SH]], 0, 0, allow_small_or_imprecise_dtypes=True))
    t_va = tok("sg", g.iota(T.VAL[:], [[1, 192]], SH, 0, allow_small_or_imprecise_dtypes=True))
    t_ms = tok("sv", V.memset(T.PT[:, 480:648], 0.0))
    need("v", t_mi)
    t_mj = tok("sv", V.tensor_scalar(T.MJ[:], T.MI[:], 15, None, AluOpType.bitwise_and))
    need("v", t_pi)
    t_pa = tok("sv", V.tensor_scalar(T.PA[:], T.PI[:], 7, None, AluOpType.bitwise_and))
    t_pb = tok("sv", V.tensor_scalar(T.PB[:], T.PI[:], 3, None, AluOpType.arith_shift_right))
    need("v", t_mj)
    t_mk = tok("sv", V.tensor_scalar(T.MK[:], T.MJ[:], 0.0, 4.0, AluOpType.is_equal, mult))
    need("v", t_pa)
    t_pf = tok("sv", V.tensor_scalar(T.PF[:], T.PA[:], 80.0, None, mult))
    need("v", t_pf, t_pb)
    t_pg = tok("sv", V.tensor_tensor(T.PG[:], T.PF[:], T.PB[:], add))
    need("v", t_pg, t_kb)
    t_lf = tok("sv", V.tensor_scalar(T.LF[:], T.KB[:], T.PG[:, 0:1], None, add))
    need("v", t_lf)
    t_ls = tok("sv", V.tensor_copy(T.LST[:], T.LF[:]))

    need("v", w_w)
    t_q0 = tok("sv", V.quantize_mx(T.C[:, base:base + SH], T.CS[:, base:base + SH], T.M[:, 0:4 * SH]))
    need("v", w_i)
    t_i16 = tok("sv", V.tensor_copy(T.I16[:], T.IDX[:]))
    t_i4 = tok("sv", V.tensor_scalar(T.I4[:], T.IDX[:, 0:4], 4, None, mult))

    def dq(k):
        need("s", w_d)
        return tok("ss", S.activation(T.DQ[:, 256 * k:256 * k + 256], T.DL[:, 256 * k:256 * k + 256], Copy, scale=0.25))

    def plane(k, t, off, *toks):
        need("v", *toks)
        a = 4 * (SH + CH * k)
        return tok("sv", V.tensor_tensor(T.M[:, a + t:a + 4 * CH:4], T.M[:, t:a].indirect(off),
                                         T.DQ[:, 256 * k + t:256 * k + 256:4], add))

    def scatter(k, *toks):
        need("v", *toks)
        return tok("sv", V.tensor_copy(T.PT[:, SH * k:SH * k + SH].indirect(T.I16[:, 4 * k:4 * k + 4]),
                                       T.VAL[:, CH * k:CH * k + CH]))

    def seg(k, *toks):
        need("s", *toks)
        return tok("ss", S.activation(T.PT[:, SH * k:SH * k + SH], T.PT[:, SH * (k - 1):SH * k], Copy))

    def look(k, gm, *toks):
        need("v", *toks)
        return tok("sv", V.tensor_tensor(gm[:], T.PT[:, SH * (k - 1):SH * k].indirect(T.I16[:, 4 * k:4 * k + 4]),
                                         T.MK[:], mult))

    def fold(rd, gm, *toks):
        need("v", *toks)
        z = None
        for k in range(4):
            z = tok("sv", V.tensor_reduce(rd[:, k:k + 1], gm[:, 16 * k:16 * k + 16], AxisListType.X, add))
        return z

    d1q = dq(0)
    sc1 = scatter(0, t_i16, t_pt, t_va)
    d1 = [plane(0, 0, T.I4[:, 0:4], t_i4, d1q, w_w)]
    sg2 = seg(1, sc1)
    d2q = dq(1)
    gm2 = look(1, T.GM2, sc1, t_mk)
    d1.append(plane(0, 1, T.I4[:, 0:4]))
    sc2 = scatter(1, sg2)
    sg3 = seg(2, sc2)
    d3q = dq(2)
    rd2 = fold(T.RD2, T.GM2, gm2)
    gm3 = look(2, T.GM3, sc2)
    d1.append(plane(0, 2, T.I4[:, 0:4]))
    sc3 = scatter(2, sg3)
    need("s", sc3, t_ms, t_ls)
    t_vp = tok("ss", S.activation(T.VP[:], T.PT[:].indirect(T.LST[:]), Copy))
    need("v", rd2)
    of2 = tok("sv", V.tensor_copy(T.OF2[:], T.RD2[:]))
    d1.append(plane(0, 3, T.I4[:, 0:4]))
    rd3 = fold(T.RD3, T.GM3, gm3)
    d2 = [plane(1, 0, T.OF2[:], of2, d2q, *d1)]
    need("v", t_vp)
    t_vt = tok("sv", V.transpose(T.VT[:], T.VP[:]))
    d2.append(plane(1, 1, T.OF2[:]))
    need("v", t_vt)
    t_ol = tok("sv", V.tensor_copy(T.OL[:], T.VT[:, 0:160:32]))
    need("v", rd3)
    of3 = tok("sv", V.tensor_copy(T.OF3[:], T.RD3[:]))
    d2.append(plane(1, 2, T.OF2[:]))
    d2.append(plane(1, 3, T.OF2[:]))
    d3 = [plane(2, 0, T.OF3[:], of3, d3q, *d2)]
    for t in range(1, 4):
        d3.append(plane(2, t, T.OF3[:]))
    need("v", *d3)
    t_qd = tok("sv", V.quantize_mx(T.C[:, base + SH:base + SLOT], T.CS[:, base + SH:base + SLOT],
                                   T.M[:, 4 * SH:4 * SLOT]))
    need("v", w_x)
    t_qx = tok("sv", V.quantize_mx(T.XC[:], T.XS[:], T.XB[:]))

    nl = [0]
    ht = helper_table(T, topo, rank)
    helpers = [ht[d] for d in dests]

    def multi(dsts, out, src, sem):
        m = topo.mask(core, dsts[0])
        ids = []
        for c in dsts:
            m &= topo.mask(core, c)
            rid, pid, _ = topo.addr(c)
            ids.append(DstId(rid=rid, pnc=pid))
        g.remote_dma_fused([RemoteDMATransfer(dst_ids=ids, dma_engine_mask=m, remote_sem=T.sem[sem], srcs=[src],
                                              dsts=[out for c in dsts])], local_sem=T.sem.lsem)
        nl[0] += len(topo.engines(core, dsts[0]))

    need("g", t_q0)
    multi(helpers, codes(T, base, base + SH), codes(T, base, base + SH), "hc")
    multi(helpers, T.CS[:, base:base + SH], T.CS[:, base:base + SH], "hs")
    need("g", t_ol)
    multi([T.cores[d] for d in dests], T.land[rank], T.OL[:], "al%d" % rank)
    need("g", t_qd)
    for d in dests:
        dst = T.cores[d]
        rid, pid, _ = topo.addr(dst)
        m = topo.mask(core, dst)
        a, b = base + SH, base + SLOT
        g.remote_dma(out_ap=codes(T, a, b), in_ap=codes(T, a, b), remote_sem=T.sem["ad%d" % rank],
                     local_sem=T.sem.lsem, pid=pid, routing_id=rid, dma_engine_mask=m)
        g.remote_dma(out_ap=T.CS[:, a:b], in_ap=T.CS[:, a:b], remote_sem=T.sem["ad%d" % rank],
                     local_sem=T.sem.lsem, pid=pid, routing_id=rid, dma_engine_mask=m)
        nl[0] += 2 * len(topo.engines(core, dst))

    def spread(q):
        for k in range(8):
            g.sync.dma_start(T.OFF[16 * k:16 * k + 16, 40 * q:40 * q + 40], T.land[q]).then_inc(T.sem["rp%d" % q], 16)

    need("y", t_ol)
    g.sync.dma_start(T.land[rank], T.OL[:]).then_inc(T.sem.own, 16)
    need("y", ("own", 16))
    spread(rank)
    for q in order:
        need("y", ("al%d" % q, len(topo.engines(T.cores[q], core))))
        spread(q)

    items = [(rank, t) for t in range(RD)] + [(q, 0) for q in order] + [(q, t) for q in order for t in range(1, RD)]
    copies, stores = [], []
    zero_toks, nst, nr = [], [0], [0]
    for j, (q, t) in enumerate(items):
        n = SH + CH * t
        bank = T["ps%d" % (j % 8)]
        a = SLOT * q
        need("p", t_qx)
        if q == rank:
            need("p", t_q0)
            if t:
                need("p", t_qd)
        else:
            hop = ht_engines(T, topo, q, core)
            need("p", ("aw%d" % q, 2 * hop))
            if t:
                need("p", ("ad%d" % q, 2 * len(topo.engines(T.cores[q], core))))
        if j >= 8:
            need("p", copies[j - 8])
        mm = tok("sp", g.tensor.matmul_mx(bank[:, 0:n], T.XC[:, 128 * t:128 * t + 128], T.XS[:, 128 * t:128 * t + 128],
                                          T.C[:, a:a + n], T.CS[:, a:a + n], True, True))
        need("s", mm)
        blk = SH * (t * NR + q)
        if t == 0:
            c = tok("ss", S.activation(T.Y[:, blk:blk + SH], bank[:, 0:n], Copy))
            copies.append(c)
            zero_toks.append(c)
            if len(zero_toks) == NR:
                need("y", *zero_toks)
                g.sync.dma_start(T.y[:, 0:NR * SH], T.Y[:, 0:NR * SH]).then_inc(T.sem.st, 16)
                nst[0] += 16
        else:
            o = SLOT * nr[0]
            nr[0] += 1
            c = tok("ss", S.activation(T.R[:, o:o + n], bank[:, 0:n], Copy))
            copies.append(c)
            need("v", c, ("rp%d" % q, 128))
            k = 40 * q + 10 * (t - 1)
            f = tok("sv", V.tensor_copy(T.Y[:, blk:blk + SH], T.R[:, o:o + n].indirect(T.OFF[:, k:k + 10])))
            need("y", f)
            g.sync.dma_start(T.y[:, blk:blk + SH], T.Y[:, blk:blk + SH]).then_inc(T.sem.st, 16)
            nst[0] += 16

    need("y", ("st", nst[0]))
    for s in ("sg", "sv", "ss", "sp"):
        need("y", (s, cnt[s]))
    need("g", ("lsem", nl[0]))


def ht_engines(T, topo, q, core):
    h = helper_table(T, topo, q)[T.rank_of(core)]
    return len(topo.engines(h, core))
